import numpy as np
import ml_dtypes


def mxq(x, axis, fmt="e4m3"):
    dtype, down = {"e4m3": (ml_dtypes.float8_e4m3fn, 7), "e5m2": (ml_dtypes.float8_e5m2, 14)}[fmt]
    v = np.moveaxis(np.asarray(x, np.float32).astype(ml_dtypes.bfloat16).astype(np.float64), axis, -1)
    blocks = v.reshape(v.shape[:-1] + (-1, 32))
    amax = np.abs(blocks).max(-1, keepdims=True)
    byte = np.maximum(np.where(amax > 0, np.frexp(amax)[1] - 1 + 127, 0) - down, 1)
    scale = np.exp2(byte - 127.0)
    codes = (blocks / scale).astype(np.float32).astype(dtype).astype(np.float64)
    return np.moveaxis((codes * scale).reshape(v.shape), -1, axis)


WIDE = False


def mx_kscale(k):
    if not WIDE:
        return np.ones(k)
    levels = np.array([10, -10, 5, -5, 0])
    if k % 512:
        return np.exp2(np.random.permutation(np.resize(levels, k // 32))).repeat(32)
    a = np.empty((k // 512, 16))
    for p in range(k // 512):
        a[p, :8] = np.random.permutation(np.resize(levels, 8))
        for g in range(8):
            far = levels[np.abs(levels - a[p, g]) >= 10]
            a[p, g + 8] = far[np.random.randint(len(far))]
    return np.exp2(a.ravel()).repeat(32)


def f64(x):
    return np.asarray(x).astype(np.float64)


def striped(idx):
    return np.tile(idx.reshape(-1, 16).T, (8, 1)).astype(np.uint16)


def unstriped(offs):
    return offs[:16].T.reshape(-1).astype(np.int64)


E2M1 = np.array([0.0, 0.5, 1.0, 1.5, 2.0, 3.0, 4.0, 6.0, -0.0, -0.5, -1.0, -1.5, -2.0, -3.0, -4.0, -6.0])


def pack_weight(w, fmt):
    k, n = w.shape
    w = f64(np.asarray(w, np.float32).astype(ml_dtypes.bfloat16)).reshape(k // 32, 32, n)
    amax = np.abs(w).max(1)
    if fmt == "e4m3":
        byte = np.frexp(amax)[1] - 1 + 127 - 7
    else:
        mant, ex = np.frexp(amax / 6.0)
        byte = np.where(mant > 0.5, ex, ex - 1) + 127
    byte = np.clip(np.where(amax > 0, byte, 1), 1, 254)
    scaled = (w * np.exp2(127.0 - byte)[:, None, :]).reshape(k, n).astype(np.float32)
    by_word = np.ascontiguousarray(scaled.reshape(k // 512, 128, 4, n).transpose(0, 1, 3, 2))
    if fmt == "e4m3":
        words = by_word.astype(ml_dtypes.float8_e4m3fn).view(np.uint8)
    else:
        c = by_word.astype(ml_dtypes.float4_e2m1fn).view(np.uint8) & 0xF
        words = (c[..., 0::2] | (c[..., 1::2] << 4)).reshape(k // 512, 128, 2 * n)
    return np.ascontiguousarray(words), np.ascontiguousarray(byte.astype(np.uint8).reshape(k // 512, 16, n))


def unpack_weight(words, scales, fmt):
    g, _, n = scales.shape
    words = np.ascontiguousarray(words).reshape(g, 128, n, -1)
    if fmt == "e4m3":
        vals = words.view(ml_dtypes.float8_e4m3fn).astype(np.float64)
    else:
        nib = np.empty((g, 128, n, 4), np.uint8)
        nib[..., 0::2] = words & 0xF
        nib[..., 1::2] = words >> 4
        vals = E2M1[nib]
    vals = vals * np.repeat(np.exp2(scales.astype(np.float64) - 127.0), 8, axis=1)[..., None]
    return vals.transpose(0, 1, 3, 2).reshape(g * 512, n)


def gelu(v):
    return 0.5 * v * (1.0 + np.tanh(np.sqrt(2.0 / np.pi) * (v + 0.044715 * v**3)))


def bf(x):
    return np.asarray(x, np.float32).astype(ml_dtypes.bfloat16)


def planes(Y):
    n, m = Y.shape
    b = f64(bf(Y)).reshape(n // 32, 32, m)
    amax = np.abs(b).max(1)
    byte = np.clip(np.where(amax > 0, np.frexp(amax)[1] - 1 + 127 - 7, 1), 1, 254)
    codes = (b * np.exp2(127.0 - byte)[:, None, :]).reshape(n, m).astype(np.float32).astype(ml_dtypes.float8_e4m3fn).view(np.uint8)
    words = codes.reshape(n // 512, 128, 4, m).transpose(0, 1, 3, 2)
    return np.ascontiguousarray(words), np.ascontiguousarray(byte.astype(np.uint8).reshape(n // 512, 16, m))


K, T, S, H, N, P = 1024, 4096, 1024, 1024, 512, 512

def setup_inputs():
    n = np.random.standard_normal
    s = mx_kscale(K)[:, None]
    u = mx_kscale(H)[:, None]
    tab_words, tab_scales = pack_weight(n((K, T)) * s, "e4m3")
    w1_words, w1_scales = pack_weight(n((K, H)) / np.sqrt(K) / s * u.T, "e2m1")
    size = np.exp(0.8 * n(N))
    return {
        "tab_words": tab_words, "tab_scales": tab_scales,
        "offs": striped(np.random.permutation(T)[:S]),
        "pos1": striped(np.random.permutation(S)[:P]),
        "pos2": striped(np.random.permutation(S)[:P]),
        "w1_words": w1_words, "w1_scales": w1_scales,
        "low": (0.5 * n(H) * u[:, 0]).astype(np.float32),
        "wa": (0.8 * n((H, N)) / np.sqrt(H) / u).astype(np.float32),
        "wb": (0.65 * n((K, N)) / np.sqrt(K) / s).astype(np.float32),
        "vib": n(N).astype(np.float32),
        "wear": (0.6 * size[:, None] * n((N, P))).astype(np.float32),
        "gain": (size * np.random.uniform(0.8, 1.6, N)).astype(np.float32),
    }

def reference(tab_words, tab_scales, offs, pos1, pos2, w1_words, w1_scales, low, wa, wb, vib, wear, gain):
    v = unpack_weight(tab_words, tab_scales, "e4m3")[:, unstriped(offs)]
    w1 = unpack_weight(w1_words, w1_scales, "e2m1")
    h = np.maximum(w1.T @ v, f64(low)[:, None])
    hq = mxq(h, 0, "e4m3")
    waq = mxq(f64(wa), 0, "e4m3")
    wbq = mxq(f64(wb), 0, "e4m3")
    e = waq.T @ hq + wbq.T @ v
    a = 1.0 / (1.0 + np.exp(-(e[:, unstriped(pos1)] + f64(vib)[:, None])))
    c = e[:, unstriped(pos2)]
    y = np.abs(a - c) * f64(wear) - f64(gain)[:, None] * a
    words, scales = planes(y)
    return y, words, scales

@@ -1,0 +1,218 @@
+from contextlib import ExitStack
+
+import concourse.mybir as mybir
+
+K, T, S, H, N, W = 1024, 4096, 1024, 1024, 512, 512
+FLOPS = 2 * K * H * S + 2 * (H + K) * N * S
+
+F32 = mybir.dt.float32
+BF16 = mybir.dt.bfloat16
+I32 = mybir.dt.int32
+U32 = mybir.dt.uint32
+U16 = mybir.dt.uint16
+U8 = mybir.dt.uint8
+E4M3 = mybir.dt.float8_e4m3fn_x4
+E2M1 = mybir.dt.float4_e2m1fn_x4
+ALU = mybir.AluOpType
+ACT = mybir.ActivationFunctionType
+
+P = 128
+PACK = 4
+PASS = P * PACK
+HALF = 512
+CHUNK = 128
+
+
+def tile_list_rotor_window_scores_kernel(
+    tc, tab_words, tab_scales, offs, pos1, pos2, w1_words, w1_scales, low, wa, wb, vib, wear, gain,
+    out_0, out_1, out_2,
+):
+    nc = tc.nc
+    with ExitStack() as ctx:
+        lists = ctx.enter_context(tc.tile_pool(name="lists", bufs=1))
+        keep = ctx.enter_context(tc.tile_pool(name="keep", bufs=1))
+        ring = ctx.enter_context(tc.tile_pool(name="ring", bufs=2))
+        psum = ctx.enter_context(tc.psum_pool(name="psum", bufs=4))
+
+        offs_sb = lists.tile([P, S // 16], U16, name="offs_sb")
+        pos1_sb = lists.tile([P, W // 16], U16, name="pos1_sb")
+        pos2_sb = lists.tile([P, W // 16], U16, name="pos2_sb")
+        nc.sync.dma_start(offs_sb[:], offs)
+
+        tab_w = [keep.tile([P, T], I32, name=f"tab_w{a}", align_bytes=64) for a in range(2)]
+        tab_s = keep.tile([P, 2, T], U8, name="tab_s", align_bytes=64)
+        w1_raw = keep.tile([P, 2, 2 * H], U8, name="w1_raw", align_bytes=64)
+        w1s_raw = keep.tile([P, 2, H], U8, name="w1s_raw", align_bytes=64)
+        tab_s_words = tab_s[:].rearrange("p a t -> p (a t)").bitcast(I32)
+        nc.vector.memset(tab_s_words[:, :1408], 0)
+        nc.gpsimd.memset(tab_s_words[:, 1408:], 0)
+        nc.gpsimd.memset(w1s_raw[:].bitcast(I32), 0)
+
+        nc.scalar.dma_start(tab_w[0][:], tab_words[0].rearrange("p t i -> p (t i)").bitcast(I32))
+        nc.sync.dma_start(w1_raw[:].bitcast(I32), w1_words.rearrange("a p c -> p a c").bitcast(I32))
+        for q in range(4):
+            nc.sync.dma_start(
+                tab_s[32 * q : 32 * q + 4, :, :].bitcast(I32),
+                tab_scales[:, 4 * q : 4 * q + 4, :].rearrange("a r t -> r a t").bitcast(I32),
+            )
+        nc.sync.dma_start(tab_w[1][:], tab_words[1].rearrange("p t i -> p (t i)").bitcast(I32))
+        for q in range(4):
+            nc.scalar.dma_start(
+                w1s_raw[32 * q : 32 * q + 4, :, :].bitcast(I32),
+                w1_scales[:, 4 * q : 4 * q + 4, :].rearrange("a r c -> r a c").bitcast(I32),
+            )
+        low_sb = keep.tile([P, 2, PACK], F32, name="low_sb")
+        vib_sb = keep.tile([P, PACK], F32, name="vib_sb")
+        gain_sb = keep.tile([P, PACK], F32, name="gain_sb")
+        nc.gpsimd.dma_start(low_sb[:], low.rearrange("(b p i) -> p b i", b=2, i=PACK))
+        nc.gpsimd.dma_start(vib_sb[:], vib.rearrange("(p t) -> p t", t=PACK))
+        nc.gpsimd.dma_start(gain_sb[:], gain.rearrange("(p t) -> p t", t=PACK))
+
+        v_s = [keep.tile([P, S], U8, name=f"v_s{a}", align_bytes=64) for a in range(2)]
+        for a in range(2):
+            nc.vector.tensor_copy(v_s[a][:], tab_s[:, a, :].indirect(offs_sb[:]))
+        v_w0 = keep.tile([P, S], U32, name="v_w0", align_bytes=64)
+        nc.vector.tensor_copy(v_w0[:], tab_w[0][:].bitcast(U32).indirect(offs_sb[:]))
+
+        w1_d = keep.tile([P, 2, 2 * H], U8, name="w1_d", align_bytes=64)
+        w1s_d = keep.tile([P, 2, H], U8, name="w1s_d", align_bytes=64)
+        nc.scalar.copy(
+            w1_d[:].bitcast(U16).rearrange("p a (b i m) -> p (a b) i m", b=2, i=PACK),
+            w1_raw[:].bitcast(U16).rearrange("p a (b m i) -> p (a b) i m", b=2, i=PACK),
+        )
+        nc.vector.tensor_copy(
+            w1s_d[:].rearrange("p a (b i m) -> p (a b) i m", b=2, i=PACK),
+            w1s_raw[:].rearrange("p a (b m i) -> p (a b) i m", b=2, i=PACK),
+        )
+        neg_gain = keep.tile([P, PACK], F32, name="neg_gain")
+        nc.vector.tensor_scalar(neg_gain[:], gain_sb[:], -1.0, None, ALU.mult)
+
+        v_w1 = [keep.tile([P, HALF], U32, name=f"v_w1{j}", align_bytes=64) for j in range(2)]
+        for j in range(2):
+            nc.vector.tensor_copy(
+                v_w1[j][:], tab_w[1][:].bitcast(U32).indirect(offs_sb[:, j * 32 : (j + 1) * 32])
+            )
+
+        def v_words(a, c0, n):
+            if a == 0:
+                return v_w0[:, c0 : c0 + n].bitcast(E4M3)
+            return v_w1[c0 // HALF][:, c0 % HALF : c0 % HALF + n].bitcast(E4M3)
+
+        raw = {}
+        for a, (name, w) in enumerate((("wb", wb), ("wa", wa))):
+            raw[name] = keep.tile([P, 2, PACK * N], F32, name=f"{name}_raw", align_bytes=64)
+            for g in range(2):
+                nc.sync.dma_start(
+                    raw[name][:, g, :], w[g * PASS : (g + 1) * PASS, :].rearrange("(p j) n -> p (j n)", j=PACK)
+                )
+        wear_sb = keep.tile([P, PACK, W], F32, name="wear_sb", align_bytes=64)
+        nc.sync.dma_start(pos1_sb[:], pos1)
+        nc.sync.dma_start(pos2_sb[:], pos2)
+        nc.sync.dma_start(wear_sb[:], wear.rearrange("(p t) m -> p t m", t=PACK))
+
+        w_codes, w_scales = {}, {}
+
+        def quantise_weight(name, g):
+            grouped = ring.tile([P, PACK * N], BF16, name="w_grouped", align_bytes=64)
+            nc.scalar.copy(
+                grouped[:].rearrange("p (t m j) -> p m t j", t=PACK, j=PACK),
+                raw[name][:, g, :].rearrange("p (j m t) -> p m t j", j=PACK, t=PACK),
+            )
+            codes = keep.tile([P, N], U32, name=f"{name}_codes{g}", align_bytes=64)
+            scales = keep.tile([P, N], U8, name=f"{name}_scales{g}", align_bytes=64)
+            nc.vector.quantize_mx(codes[:].bitcast(E4M3), scales[:], grouped[:])
+            w_codes[name, g], w_scales[name, g] = codes, scales
+
+        h_codes, h_scales = {}, {}
+        weight_order = [("wb", 0), ("wb", 1), ("wa", 0), ("wa", 1)]
+        for u, (j, b) in enumerate([(j, b) for j in range(2) for b in range(2)]):
+            h_bf = ring.tile([P, HALF, PACK], BF16, name="h_bf", align_bytes=64)
+            for c in range(HALF // CHUNK):
+                bank = psum.tile([P, PACK, CHUNK], F32, name="h_bank")
+                c0 = j * HALF + c * CHUNK
+                for a in range(2):
+                    for i in range(PACK):
+                        col = b * PASS + i * P
+                        nc.tensor.matmul_mx(
+                            out=bank[:, i, :],
+                            lhsT=w1_d[:, a, 2 * col : 2 * (col + P)].bitcast(E2M1),
+                            lhsT_scale=w1s_d[:, a, col : col + P],
+                            rhs=v_words(a, c0, CHUNK),
+                            rhs_scale=v_s[a][:, c0 : c0 + CHUNK],
+                            start=(a == 0 and i == 0),
+                            stop=(a == 1 and i == PACK - 1),
+                        )
+                nc.vector.tensor_tensor(
+                    h_bf[:, c * CHUNK : (c + 1) * CHUNK, :],
+                    bank[:].rearrange("p i n -> p n i"),
+                    low_sb[:, b : b + 1, :].to_broadcast([P, CHUNK, PACK]),
+                    ALU.max,
+                )
+            codes = keep.tile([P, HALF], U32, name=f"h_codes{u}", align_bytes=64)
+            scales = keep.tile([P, HALF], U8, name=f"h_scales{u}", align_bytes=64)
+            nc.vector.quantize_mx(codes[:].bitcast(E4M3), scales[:], h_bf[:].rearrange("p n i -> p (n i)"))
+            h_codes[j, b], h_scales[j, b] = codes, scales
+            quantise_weight(*weight_order[u])
+
+        y = keep.tile([P, PACK, W], F32, name="y", align_bytes=64)
+        out_rows = out_0.rearrange("(p t) m -> p t m", t=PACK)
+        e = [keep.tile([P, S], F32, name=f"e{t}", align_bytes=64) for t in range(PACK)]
+
+        def scores(t):
+            cols = slice(t * P, (t + 1) * P)
+            for j in range(2):
+                bank = psum.tile([P, HALF], F32, name="e_bank", tag="e_bank" if t < 2 else "h_bank")
+                passes = [
+                    ("wb", g, v_words(g, j * HALF, HALF), v_s[g][:, j * HALF : (j + 1) * HALF]) for g in range(2)
+                ] + [("wa", g, h_codes[j, g][:].bitcast(E4M3), h_scales[j, g][:]) for g in range(2)]
+                for n, (name, g, rhs, rhs_scale) in enumerate(passes):
+                    nc.tensor.matmul_mx(
+                        out=bank[:],
+                        lhsT=w_codes[name, g][:, cols].bitcast(E4M3),
+                        lhsT_scale=w_scales[name, g][:, cols],
+                        rhs=rhs,
+                        rhs_scale=rhs_scale,
+                        start=(n == 0),
+                        stop=(n == len(passes) - 1),
+                    )
+                if j == 1 and t < 2:
+                    nc.vector.tensor_copy(e[t][:, j * HALF : (j + 1) * HALF], bank[:])
+                else:
+                    nc.scalar.copy(e[t][:, j * HALF : (j + 1) * HALF], bank[:])
+
+        gate, gap = {}, {}
+
+        def look(t):
+            gate[t] = keep.tile([P, W], F32, name=f"gate{t}")
+            nc.scalar.activation(gate[t][:], e[t][:].indirect(pos1_sb[:]), ACT.Sigmoid, bias=vib_sb[:, t : t + 1])
+            diff = keep.tile([P, W], F32, name=f"diff{t}")
+            nc.vector.tensor_tensor(diff[:], e[t][:].indirect(pos2_sb[:]), gate[t][:], ALU.subtract)
+            gap[t] = keep.tile([P, W], F32, name=f"gap{t}")
+            nc.scalar.activation(gap[t][:], diff[:], ACT.Abs)
+
+        def finish(t):
+            weighted = ring.tile([P, W], F32, name="weighted")
+            nc.vector.tensor_tensor(weighted[:], gap[t][:], wear_sb[:, t, :], ALU.mult)
+            nc.vector.scalar_tensor_tensor(
+                y[:, t, :], gate[t][:], neg_gain[:, t : t + 1], weighted[:], ALU.mult, ALU.add
+            )
+            nc.sync.dma_start(out_rows[:, t, :], y[:, t, :])
+
+        for t in range(PACK + 1):
+            if t < PACK:
+                scores(t)
+                look(t)
+            if t > 0:
+                finish(t - 1)
+
+        y_bf = keep.tile([P, W, PACK], BF16, name="y_bf", align_bytes=64)
+        nc.vector.tensor_copy(y_bf[:], y[:].rearrange("p t m -> p m t"))
+        y_codes = keep.tile([P, W], U32, name="y_codes", align_bytes=64)
+        y_scales = keep.tile([P, W], U8, name="y_scales", align_bytes=64)
+        nc.vector.quantize_mx(y_codes[:].bitcast(E4M3), y_scales[:], y_bf[:].rearrange("p m t -> p (m t)"))
+        nc.sync.dma_start(out_1[0].rearrange("p m t -> p (m t)").bitcast(I32), y_codes[:].bitcast(I32))
+        for q in range(4):
+            queue = nc.scalar if q % 2 == 0 else nc.sync
+            queue.dma_start(
+                out_2[0, 4 * q : 4 * q + 4, :].bitcast(I32), y_scales[32 * q : 32 * q + 4, :].bitcast(I32)
+            )

@@ -32,88 +32,95 @@ def tile_list_rotor_window_scores_kernel(
         lists = ctx.enter_context(tc.tile_pool(name="lists", bufs=1))
         keep = ctx.enter_context(tc.tile_pool(name="keep", bufs=1))
         ring = ctx.enter_context(tc.tile_pool(name="ring", bufs=2))
-        psum = ctx.enter_context(tc.psum_pool(name="psum", bufs=4))
+        psum = ctx.enter_context(tc.psum_pool(name="psum", bufs=1))
 
         offs_sb = lists.tile([P, S // 16], U16, name="offs_sb")
         pos1_sb = lists.tile([P, W // 16], U16, name="pos1_sb")
         pos2_sb = lists.tile([P, W // 16], U16, name="pos2_sb")
         nc.sync.dma_start(offs_sb[:], offs)
 
-        tab_w = [keep.tile([P, T], I32, name=f"tab_w{a}", align_bytes=64) for a in range(2)]
-        tab_s = keep.tile([P, 2, T], U8, name="tab_s", align_bytes=64)
+        tab_s = keep.tile([P, T], U8, name="tab_s", align_bytes=64)
+        w1s_raw = keep.tile([P, H], U8, name="w1s_raw", align_bytes=64)
         w1_raw = keep.tile([P, 2, 2 * H], U8, name="w1_raw", align_bytes=64)
-        w1s_raw = keep.tile([P, 2, H], U8, name="w1s_raw", align_bytes=64)
-        tab_s_words = tab_s[:].rearrange("p a t -> p (a t)").bitcast(I32)
-        nc.vector.memset(tab_s_words[:, :1408], 0)
-        nc.gpsimd.memset(tab_s_words[:, 1408:], 0)
-        nc.gpsimd.memset(w1s_raw[:].bitcast(I32), 0)
-
-        nc.scalar.dma_start(tab_w[0][:], tab_words[0].rearrange("p t i -> p (t i)").bitcast(I32))
+        planes = [keep.tile([P, S + H], U8, name=f"planes{a}", align_bytes=64) for a in range(2)]
+        tab_w0 = keep.tile([P, T], I32, name="tab_w0", align_bytes=64)
+        nc.sync.dma_start(tab_s[0:32, :].bitcast(I32), tab_scales.rearrange("a q t -> (a q) t").bitcast(I32))
+        nc.sync.dma_start(w1s_raw[0:32, :].bitcast(I32), w1_scales.rearrange("a q c -> (a q) c").bitcast(I32))
         nc.sync.dma_start(w1_raw[:].bitcast(I32), w1_words.rearrange("a p c -> p a c").bitcast(I32))
-        for q in range(4):
-            nc.sync.dma_start(
-                tab_s[32 * q : 32 * q + 4, :, :].bitcast(I32),
-                tab_scales[:, 4 * q : 4 * q + 4, :].rearrange("a r t -> r a t").bitcast(I32),
-            )
-        nc.sync.dma_start(tab_w[1][:], tab_words[1].rearrange("p t i -> p (t i)").bitcast(I32))
-        for q in range(4):
-            nc.scalar.dma_start(
-                w1s_raw[32 * q : 32 * q + 4, :, :].bitcast(I32),
-                w1_scales[:, 4 * q : 4 * q + 4, :].rearrange("a r c -> r a c").bitcast(I32),
-            )
-        low_sb = keep.tile([P, 2, PACK], F32, name="low_sb")
-        vib_sb = keep.tile([P, PACK], F32, name="vib_sb")
-        gain_sb = keep.tile([P, PACK], F32, name="gain_sb")
-        nc.gpsimd.dma_start(low_sb[:], low.rearrange("(b p i) -> p b i", b=2, i=PACK))
-        nc.gpsimd.dma_start(vib_sb[:], vib.rearrange("(p t) -> p t", t=PACK))
-        nc.gpsimd.dma_start(gain_sb[:], gain.rearrange("(p t) -> p t", t=PACK))
+        nc.sync.dma_start(tab_w0[:], tab_words[0].rearrange("p t i -> p (t i)").bitcast(I32))
+        for rows in (slice(32, 64), slice(64, P)):
+            nc.vector.memset(tab_s[rows, :].bitcast(I32), 0)
+            nc.gpsimd.memset(w1s_raw[rows, :].bitcast(I32), 0)
+        nc.gpsimd.memset(planes[1][:].bitcast(I32), 0)
 
-        v_s = [keep.tile([P, S], U8, name=f"v_s{a}", align_bytes=64) for a in range(2)]
-        for a in range(2):
-            nc.vector.tensor_copy(v_s[a][:], tab_s[:, a, :].indirect(offs_sb[:]))
-        v_w0 = keep.tile([P, S], U32, name="v_w0", align_bytes=64)
-        nc.vector.tensor_copy(v_w0[:], tab_w[0][:].bitcast(U32).indirect(offs_sb[:]))
+        low_sb = keep.tile([P, 2, 2 * PACK], F32, name="low_sb")
+        low_runs = low.rearrange("(b k x) -> k b x", b=2, x=2 * PACK)
+        for e in range(2):
+            nc.gpsimd.dma_start(low_sb[e:P:2, :, 0:7], low_runs[:, :, e : e + 7])
+
+        picked_s = keep.tile([P, S], U8, name="picked_s", align_bytes=64)
+        nc.vector.tensor_copy(picked_s[:], tab_s[:].indirect(offs_sb[:]))
+        nc.vector.tensor_copy(planes[0][:, :S].bitcast(I32), picked_s[:].bitcast(I32))
+        nc.scalar.copy(
+            planes[0][:, S:].bitcast(U16).rearrange("p (b i k) -> p b k i", b=2, i=PACK),
+            w1s_raw[:].bitcast(U16).rearrange("p (b k i) -> p b k i", b=2, i=PACK),
+        )
+        for q in range(1, 4):
+            nc.sync.dma_start(
+                planes[0][32 * q : 32 * q + 4, :].bitcast(I32), planes[0][4 * q : 4 * q + 4, :].bitcast(I32)
+            )
+        for q in range(4):
+            (nc.gpsimd if q == 0 else nc.sync).dma_start(
+                planes[1][32 * q : 32 * q + 4, :].bitcast(I32),
+                planes[0][16 + 4 * q : 20 + 4 * q, :].bitcast(I32),
+            )
+        tab_w1 = keep.tile([P, T], I32, name="tab_w1", align_bytes=64)
+        nc.sync.dma_start(tab_w1[:], tab_words[1].rearrange("p t i -> p (t i)").bitcast(I32))
 
         w1_d = keep.tile([P, 2, 2 * H], U8, name="w1_d", align_bytes=64)
-        w1s_d = keep.tile([P, 2, H], U8, name="w1s_d", align_bytes=64)
         nc.scalar.copy(
-            w1_d[:].bitcast(U16).rearrange("p a (b i m) -> p (a b) i m", b=2, i=PACK),
-            w1_raw[:].bitcast(U16).rearrange("p a (b m i) -> p (a b) i m", b=2, i=PACK),
+            w1_d[:].bitcast(U32).rearrange("p a (b i k) -> p (a b) k i", b=2, i=PACK),
+            w1_raw[:].bitcast(U32).rearrange("p a (b k i) -> p (a b) k i", b=2, i=PACK),
         )
-        nc.vector.tensor_copy(
-            w1s_d[:].rearrange("p a (b i m) -> p (a b) i m", b=2, i=PACK),
-            w1s_raw[:].rearrange("p a (b m i) -> p (a b) i m", b=2, i=PACK),
-        )
-        neg_gain = keep.tile([P, PACK], F32, name="neg_gain")
-        nc.vector.tensor_scalar(neg_gain[:], gain_sb[:], -1.0, None, ALU.mult)
 
-        v_w1 = [keep.tile([P, HALF], U32, name=f"v_w1{j}", align_bytes=64) for j in range(2)]
-        for j in range(2):
-            nc.vector.tensor_copy(
-                v_w1[j][:], tab_w[1][:].bitcast(U32).indirect(offs_sb[:, j * 32 : (j + 1) * 32])
-            )
+        v_w = {}
+        for a, tab_w in enumerate((tab_w0, tab_w1)):
+            for j in range(2):
+                v_w[a, j] = keep.tile([P, HALF], U32, name=f"v_w{a}{j}", align_bytes=64)
+                nc.vector.tensor_copy(
+                    v_w[a, j][:], tab_w[:].bitcast(U32).indirect(offs_sb[:, j * 32 : (j + 1) * 32])
+                )
 
         def v_words(a, c0, n):
-            if a == 0:
-                return v_w0[:, c0 : c0 + n].bitcast(E4M3)
-            return v_w1[c0 // HALF][:, c0 % HALF : c0 % HALF + n].bitcast(E4M3)
+            return v_w[a, c0 // HALF][:, c0 % HALF : c0 % HALF + n].bitcast(E4M3)
 
-        raw = {}
-        for a, (name, w) in enumerate((("wb", wb), ("wa", wa))):
-            raw[name] = keep.tile([P, 2, PACK * N], F32, name=f"{name}_raw", align_bytes=64)
-            for g in range(2):
-                nc.sync.dma_start(
-                    raw[name][:, g, :], w[g * PASS : (g + 1) * PASS, :].rearrange("(p j) n -> p (j n)", j=PACK)
-                )
-        wear_sb = keep.tile([P, PACK, W], F32, name="wear_sb", align_bytes=64)
+        raw = {name: keep.tile([P, 2, PACK * N], F32, name=f"{name}_raw", align_bytes=64) for name in ("wb", "wa")}
+        for g in range(2):
+            nc.sync.dma_start(
+                raw["wb"][:, g, :], wb[g * PASS : (g + 1) * PASS, :].rearrange("(p j) n -> p (j n)", j=PACK)
+            )
+        for g in range(2):
+            wa_rows = wa[g * PASS : (g + 1) * PASS, :].rearrange("(k i e) n -> e k i n", i=PACK, e=2)
+            for e in range(2):
+                nc.sync.dma_start(raw["wa"][e:P:2, g, :].rearrange("p (i n) -> p i n", i=PACK), wa_rows[e])
+        vib_sb = keep.tile([P, PACK], F32, name="vib_sb")
+        gain_sb = keep.tile([P, PACK], F32, name="gain_sb")
+        nc.sync.dma_start(vib_sb[:], vib.rearrange("(p t) -> p t", t=PACK))
+        nc.sync.dma_start(gain_sb[:], gain.rearrange("(p t) -> p t", t=PACK))
         nc.sync.dma_start(pos1_sb[:], pos1)
         nc.sync.dma_start(pos2_sb[:], pos2)
+        wear_sb = keep.tile([P, PACK, W], F32, name="wear_sb", align_bytes=64)
         nc.sync.dma_start(wear_sb[:], wear.rearrange("(p t) m -> p t m", t=PACK))
+        neg_gain = keep.tile([P, PACK], F32, name="neg_gain")
+        nc.gpsimd.tensor_scalar(neg_gain[:], gain_sb[:], -1.0, 0.0, ALU.mult, ALU.add)
 
         w_codes, w_scales = {}, {}
 
         def quantise_weight(name, g):
-            grouped = ring.tile([P, PACK * N], BF16, name="w_grouped", align_bytes=64)
+            if (name, g) == ("wa", 1):
+                grouped = keep.tile([P, PACK * N], BF16, name="w_grouped_last", tag="last", align_bytes=64)
+            else:
+                grouped = ring.tile([P, PACK * N], BF16, name="w_grouped", align_bytes=64)
             nc.scalar.copy(
                 grouped[:].rearrange("p (t m j) -> p m t j", t=PACK, j=PACK),
                 raw[name][:, g, :].rearrange("p (j m t) -> p m t j", j=PACK, t=PACK),
@@ -123,51 +130,78 @@ def tile_list_rotor_window_scores_kernel(
             nc.vector.quantize_mx(codes[:].bitcast(E4M3), scales[:], grouped[:])
             w_codes[name, g], w_scales[name, g] = codes, scales
 
-        h_codes, h_scales = {}, {}
-        weight_order = [("wb", 0), ("wb", 1), ("wa", 0), ("wa", 1)]
-        for u, (j, b) in enumerate([(j, b) for j in range(2) for b in range(2)]):
-            h_bf = ring.tile([P, HALF, PACK], BF16, name="h_bf", align_bytes=64)
-            for c in range(HALF // CHUNK):
-                bank = psum.tile([P, PACK, CHUNK], F32, name="h_bank")
-                c0 = j * HALF + c * CHUNK
+        h_parts = {}
+
+        def quantise_h(j, b, n0, h_bf):
+            width = h_bf.shape[1]
+            codes = keep.tile([P, width], U32, name=f"h_codes{j}{b}_{n0}", align_bytes=64)
+            scales = keep.tile([P, width], U8, name=f"h_scales{j}{b}_{n0}", align_bytes=64)
+            nc.vector.quantize_mx(codes[:].bitcast(E4M3), scales[:], h_bf[:].rearrange("p n i -> p (n i)"))
+            h_parts.setdefault((j, b), []).append((n0, width, codes, scales))
+
+        units = [
+            (0, 0, 0, HALF, None),
+            (0, 1, 0, HALF, ("wb", 0)),
+            (1, 0, 0, HALF, ("wb", 1)),
+            (1, 1, 0, HALF // 2, ("wa", 0)),
+            (1, 1, HALF // 2, HALF // 2, ("wa", 1)),
+        ]
+        previous = None
+        n_bank = 0
+        for u, (j, b, n0, width, weight) in enumerate(units):
+            if weight is not None:
+                quantise_weight(*weight)
+            if u == len(units) - 1:
+                h_bf = keep.tile([P, width, PACK], BF16, name="h_bf_last", tag="last", align_bytes=64)
+            else:
+                h_bf = ring.tile([P, width, PACK], BF16, name="h_bf", align_bytes=64)
+            for c in range(width // CHUNK):
+                bank = psum.tile([P, PACK, CHUNK], F32, name="h_bank", tag=f"bank{n_bank if n_bank < 8 else n_bank % 4}")
+                n_bank += 1
+                c0 = j * HALF + n0 + c * CHUNK
                 for a in range(2):
                     for i in range(PACK):
                         col = b * PASS + i * P
                         nc.tensor.matmul_mx(
                             out=bank[:, i, :],
                             lhsT=w1_d[:, a, 2 * col : 2 * (col + P)].bitcast(E2M1),
-                            lhsT_scale=w1s_d[:, a, col : col + P],
+                            lhsT_scale=planes[a][:, S + col : S + col + P],
                             rhs=v_words(a, c0, CHUNK),
-                            rhs_scale=v_s[a][:, c0 : c0 + CHUNK],
+                            rhs_scale=planes[a][:, c0 : c0 + CHUNK],
                             start=(a == 0 and i == 0),
                             stop=(a == 1 and i == PACK - 1),
                         )
                 nc.vector.tensor_tensor(
                     h_bf[:, c * CHUNK : (c + 1) * CHUNK, :],
                     bank[:].rearrange("p i n -> p n i"),
-                    low_sb[:, b : b + 1, :].to_broadcast([P, CHUNK, PACK]),
+                    low_sb[:, b : b + 1, 0:7:2].to_broadcast([P, CHUNK, PACK]),
                     ALU.max,
                 )
-            codes = keep.tile([P, HALF], U32, name=f"h_codes{u}", align_bytes=64)
-            scales = keep.tile([P, HALF], U8, name=f"h_scales{u}", align_bytes=64)
-            nc.vector.quantize_mx(codes[:].bitcast(E4M3), scales[:], h_bf[:].rearrange("p n i -> p (n i)"))
-            h_codes[j, b], h_scales[j, b] = codes, scales
-            quantise_weight(*weight_order[u])
+                if c == 0 and previous is not None:
+                    quantise_h(*previous)
+            previous = (j, b, n0, h_bf)
+        quantise_h(*previous)
 
         y = keep.tile([P, PACK, W], F32, name="y", align_bytes=64)
         out_rows = out_0.rearrange("(p t) m -> p t m", t=PACK)
-        e = [keep.tile([P, S], F32, name=f"e{t}", align_bytes=64) for t in range(PACK)]
+        e = {}
 
         def scores(t):
+            e[t] = ring.tile([P, S], F32, name="e", align_bytes=64)
             cols = slice(t * P, (t + 1) * P)
             for j in range(2):
-                bank = psum.tile([P, HALF], F32, name="e_bank", tag="e_bank" if t < 2 else "h_bank")
+                bank = psum.tile([P, HALF], F32, name="e_bank", tag=f"bank{(4, 5, 6, 7, 2, 3, 5, 7)[2 * t + j]}")
                 passes = [
-                    ("wb", g, v_words(g, j * HALF, HALF), v_s[g][:, j * HALF : (j + 1) * HALF]) for g in range(2)
-                ] + [("wa", g, h_codes[j, g][:].bitcast(E4M3), h_scales[j, g][:]) for g in range(2)]
-                for n, (name, g, rhs, rhs_scale) in enumerate(passes):
+                    ("wb", g, 0, HALF, v_words(g, j * HALF, HALF), planes[g][:, j * HALF : (j + 1) * HALF])
+                    for g in range(2)
+                ] + [
+                    ("wa", g, n0, width, codes[:].bitcast(E4M3), scales[:])
+                    for g in range(2)
+                    for n0, width, codes, scales in h_parts[j, g]
+                ]
+                for n, (name, g, n0, width, rhs, rhs_scale) in enumerate(passes):
                     nc.tensor.matmul_mx(
-                        out=bank[:],
+                        out=bank[:, n0 : n0 + width],
                         lhsT=w_codes[name, g][:, cols].bitcast(E4M3),
                         lhsT_scale=w_scales[name, g][:, cols],
                         rhs=rhs,
@@ -186,27 +220,40 @@ def tile_list_rotor_window_scores_kernel(
             gate[t] = keep.tile([P, W], F32, name=f"gate{t}")
             nc.scalar.activation(gate[t][:], e[t][:].indirect(pos1_sb[:]), ACT.Sigmoid, bias=vib_sb[:, t : t + 1])
             diff = keep.tile([P, W], F32, name=f"diff{t}")
-            nc.vector.tensor_tensor(diff[:], e[t][:].indirect(pos2_sb[:]), gate[t][:], ALU.subtract)
+            if t == 0:
+                plain = keep.tile([P, W], F32, name="plain")
+                nc.vector.tensor_copy(plain[:], e[t][:].indirect(pos2_sb[:]))
+                nc.vector.tensor_tensor(diff[:], plain[:], gate[t][:], ALU.subtract)
+            else:
+                nc.vector.tensor_tensor(diff[:], e[t][:].indirect(pos2_sb[:]), gate[t][:], ALU.subtract)
             gap[t] = keep.tile([P, W], F32, name=f"gap{t}")
             nc.scalar.activation(gap[t][:], diff[:], ACT.Abs)
 
+        weighted = {}
+
+        def weigh(t):
+            weighted[t] = keep.tile([P, W], F32, name=f"weighted{t}")
+            nc.vector.tensor_tensor(weighted[t][:], gap[t][:], wear_sb[:, t, :], ALU.mult)
+
         def finish(t):
-            weighted = ring.tile([P, W], F32, name="weighted")
-            nc.vector.tensor_tensor(weighted[:], gap[t][:], wear_sb[:, t, :], ALU.mult)
             nc.vector.scalar_tensor_tensor(
-                y[:, t, :], gate[t][:], neg_gain[:, t : t + 1], weighted[:], ALU.mult, ALU.add
+                y[:, t, :], gate[t][:], neg_gain[:, t : t + 1], weighted[t][:], ALU.mult, ALU.add
             )
             nc.sync.dma_start(out_rows[:, t, :], y[:, t, :])
 
-        for t in range(PACK + 1):
-            if t < PACK:
-                scores(t)
-                look(t)
-            if t > 0:
-                finish(t - 1)
-
         y_bf = keep.tile([P, W, PACK], BF16, name="y_bf", align_bytes=64)
-        nc.vector.tensor_copy(y_bf[:], y[:].rearrange("p t m -> p m t"))
+        y_by_column = y[:].rearrange("p t m -> p m t")
+        for step in range(PACK + 2):
+            if step < PACK:
+                scores(step)
+                look(step)
+            if step >= 2:
+                finish(step - 2)
+            if 1 <= step <= PACK:
+                weigh(step - 1)
+            if step == 3:
+                nc.scalar.copy(y_bf[:, :, 0:2], y_by_column[:, :, 0:2])
+        nc.vector.tensor_copy(y_bf[:, :, 2:4], y_by_column[:, :, 2:4])
         y_codes = keep.tile([P, W], U32, name="y_codes", align_bytes=64)
         y_scales = keep.tile([P, W], U8, name="y_scales", align_bytes=64)
         nc.vector.quantize_mx(y_codes[:].bitcast(E4M3), y_scales[:], y_bf[:].rearrange("p m t -> p (m t)"))

@@ -39,6 +39,11 @@ def tile_list_rotor_window_scores_kernel(
         pos2_sb = lists.tile([P, W // 16], U16, name="pos2_sb")
         nc.sync.dma_start(offs_sb[:], offs)
 
+        warm_in = keep.tile([P, 1], F32, name="warm_in")
+        warm_out = keep.tile([P, 1], F32, name="warm_out")
+        nc.gpsimd.memset(warm_in[:], 0.0)
+        nc.scalar.activation(warm_out[:], warm_in[:], ACT.Sigmoid)
+
         tab_s = keep.tile([P, T], U8, name="tab_s", align_bytes=64)
         w1s_raw = keep.tile([P, H], U8, name="w1s_raw", align_bytes=64)
         w1_raw = keep.tile([P, 2, 2 * H], U8, name="w1_raw", align_bytes=64)

@@ -21,6 +21,7 @@ PACK = 4
 PASS = P * PACK
 HALF = 512
 CHUNK = 128
+VECTOR_COLUMNS = 320
 
 
 def tile_list_rotor_window_scores_kernel(
@@ -46,13 +47,17 @@ def tile_list_rotor_window_scores_kernel(
 
         tab_s = keep.tile([P, T], U8, name="tab_s", align_bytes=64)
         w1s_raw = keep.tile([P, H], U8, name="w1s_raw", align_bytes=64)
-        w1_raw = keep.tile([P, 2, 2 * H], U8, name="w1_raw", align_bytes=64)
+        w1_raw = [keep.tile([P, 2, 2 * PASS], U8, name=f"w1_raw{b}", align_bytes=64) for b in range(2)]
+        w1_halves = w1_words.rearrange("a p (b c) -> b p a c", b=2)
         planes = [keep.tile([P, S + H], U8, name=f"planes{a}", align_bytes=64) for a in range(2)]
         tab_w0 = keep.tile([P, T], I32, name="tab_w0", align_bytes=64)
+        tab_w1 = keep.tile([P, T], I32, name="tab_w1", align_bytes=64)
+        tab_words1 = tab_words[1].rearrange("p t i -> p (t i)").bitcast(I32)
         nc.sync.dma_start(tab_s[0:32, :].bitcast(I32), tab_scales.rearrange("a q t -> (a q) t").bitcast(I32))
         nc.sync.dma_start(w1s_raw[0:32, :].bitcast(I32), w1_scales.rearrange("a q c -> (a q) c").bitcast(I32))
-        nc.sync.dma_start(w1_raw[:].bitcast(I32), w1_words.rearrange("a p c -> p a c").bitcast(I32))
+        nc.sync.dma_start(w1_raw[0][:].bitcast(I32), w1_halves[0].bitcast(I32))
         nc.sync.dma_start(tab_w0[:], tab_words[0].rearrange("p t i -> p (t i)").bitcast(I32))
+        nc.sync.dma_start(tab_w1[:, : T // 2], tab_words1[:, : T // 2])
         for rows in (slice(32, 64), slice(64, P)):
             nc.vector.memset(tab_s[rows, :].bitcast(I32), 0)
             nc.gpsimd.memset(w1s_raw[rows, :].bitcast(I32), 0)
@@ -79,14 +84,15 @@ def tile_list_rotor_window_scores_kernel(
                 planes[1][32 * q : 32 * q + 4, :].bitcast(I32),
                 planes[0][16 + 4 * q : 20 + 4 * q, :].bitcast(I32),
             )
-        tab_w1 = keep.tile([P, T], I32, name="tab_w1", align_bytes=64)
-        nc.sync.dma_start(tab_w1[:], tab_words[1].rearrange("p t i -> p (t i)").bitcast(I32))
+        nc.sync.dma_start(tab_w1[:, T // 2 :], tab_words1[:, T // 2 :])
+        nc.sync.dma_start(w1_raw[1][:].bitcast(I32), w1_halves[1].bitcast(I32))
 
-        w1_d = keep.tile([P, 2, 2 * H], U8, name="w1_d", align_bytes=64)
-        nc.scalar.copy(
-            w1_d[:].bitcast(U32).rearrange("p a (b i k) -> p (a b) k i", b=2, i=PACK),
-            w1_raw[:].bitcast(U32).rearrange("p a (b k i) -> p (a b) k i", b=2, i=PACK),
-        )
+        w1_d = [keep.tile([P, 2, 2 * PASS], U8, name=f"w1_d{b}", align_bytes=64) for b in range(2)]
+        for b in range(2):
+            nc.scalar.copy(
+                w1_d[b][:].bitcast(U32).rearrange("p a (i k) -> p a k i", i=PACK),
+                w1_raw[b][:].bitcast(U32).rearrange("p a (k i) -> p a k i", i=PACK),
+            )
 
         v_w = {}
         for a, tab_w in enumerate((tab_w0, tab_w1)):
@@ -99,15 +105,19 @@ def tile_list_rotor_window_scores_kernel(
         def v_words(a, c0, n):
             return v_w[a, c0 // HALF][:, c0 % HALF : c0 % HALF + n].bitcast(E4M3)
 
-        raw = {name: keep.tile([P, 2, PACK * N], F32, name=f"{name}_raw", align_bytes=64) for name in ("wb", "wa")}
+        raw = {
+            (name, g): keep.tile([P, PACK * N], F32, name=f"{name}_raw{g}", tag=f"{name}_raw{g}", align_bytes=64)
+            for name in ("wb", "wa")
+            for g in range(2)
+        }
         for g in range(2):
             nc.sync.dma_start(
-                raw["wb"][:, g, :], wb[g * PASS : (g + 1) * PASS, :].rearrange("(p j) n -> p (j n)", j=PACK)
+                raw["wb", g][:], wb[g * PASS : (g + 1) * PASS, :].rearrange("(p j) n -> p (j n)", j=PACK)
             )
         for g in range(2):
             wa_rows = wa[g * PASS : (g + 1) * PASS, :].rearrange("(k i e) n -> e k i n", i=PACK, e=2)
             for e in range(2):
-                nc.sync.dma_start(raw["wa"][e:P:2, g, :].rearrange("p (i n) -> p i n", i=PACK), wa_rows[e])
+                nc.sync.dma_start(raw["wa", g][e:P:2, :].rearrange("p (i n) -> p i n", i=PACK), wa_rows[e])
         vib_sb = keep.tile([P, PACK], F32, name="vib_sb")
         gain_sb = keep.tile([P, PACK], F32, name="gain_sb")
         nc.sync.dma_start(vib_sb[:], vib.rearrange("(p t) -> p t", t=PACK))
@@ -119,21 +129,21 @@ def tile_list_rotor_window_scores_kernel(
         neg_gain = keep.tile([P, PACK], F32, name="neg_gain")
         nc.gpsimd.tensor_scalar(neg_gain[:], gain_sb[:], -1.0, 0.0, ALU.mult, ALU.add)
 
-        w_codes, w_scales = {}, {}
+        grouped, w_codes, w_scales = {}, {}, {}
+        early = (PACK - 1) * P
 
         def quantise_weight(name, g):
-            if (name, g) == ("wa", 1):
-                grouped = keep.tile([P, PACK * N], BF16, name="w_grouped_last", tag="last", align_bytes=64)
-            else:
-                grouped = ring.tile([P, PACK * N], BF16, name="w_grouped", align_bytes=64)
+            grouped[name, g] = keep.tile([P, PACK * N], BF16, name=f"{name}_grouped{g}", align_bytes=64)
             nc.scalar.copy(
-                grouped[:].rearrange("p (t m j) -> p m t j", t=PACK, j=PACK),
-                raw[name][:, g, :].rearrange("p (j m t) -> p m t j", j=PACK, t=PACK),
+                grouped[name, g][:].rearrange("p (t m j) -> p m j t", t=PACK, j=PACK),
+                raw[name, g][:].rearrange("p (j m t) -> p m j t", j=PACK, t=PACK),
             )
-            codes = keep.tile([P, N], U32, name=f"{name}_codes{g}", align_bytes=64)
-            scales = keep.tile([P, N], U8, name=f"{name}_scales{g}", align_bytes=64)
-            nc.vector.quantize_mx(codes[:].bitcast(E4M3), scales[:], grouped[:])
-            w_codes[name, g], w_scales[name, g] = codes, scales
+            codes = keep.tile([P, early], U32, name=f"{name}_codes{g}", align_bytes=64)
+            scales = keep.tile([P, early], U8, name=f"{name}_scales{g}", align_bytes=64)
+            nc.vector.quantize_mx(codes[:].bitcast(E4M3), scales[:], grouped[name, g][:, : PACK * early])
+            for t in range(PACK - 1):
+                w_codes[name, g, t] = codes[:, t * P : (t + 1) * P]
+                w_scales[name, g, t] = scales[:, t * P : (t + 1) * P]
 
         h_parts = {}
 
@@ -146,8 +156,8 @@ def tile_list_rotor_window_scores_kernel(
 
         units = [
             (0, 0, 0, HALF, None),
-            (0, 1, 0, HALF, ("wb", 0)),
-            (1, 0, 0, HALF, ("wb", 1)),
+            (1, 0, 0, HALF, ("wb", 0)),
+            (0, 1, 0, HALF, ("wb", 1)),
             (1, 1, 0, HALF // 2, ("wa", 0)),
             (1, 1, HALF // 2, HALF // 2, ("wa", 1)),
         ]
@@ -157,7 +167,7 @@ def tile_list_rotor_window_scores_kernel(
             if weight is not None:
                 quantise_weight(*weight)
             if u == len(units) - 1:
-                h_bf = keep.tile([P, width, PACK], BF16, name="h_bf_last", tag="last", align_bytes=64)
+                h_bf = keep.tile([P, width, PACK], BF16, name="h_bf_last", tag="wa_raw1", align_bytes=64)
             else:
                 h_bf = ring.tile([P, width, PACK], BF16, name="h_bf", align_bytes=64)
             for c in range(width // CHUNK):
@@ -169,7 +179,7 @@ def tile_list_rotor_window_scores_kernel(
                         col = b * PASS + i * P
                         nc.tensor.matmul_mx(
                             out=bank[:, i, :],
-                            lhsT=w1_d[:, a, 2 * col : 2 * (col + P)].bitcast(E2M1),
+                            lhsT=w1_d[b][:, a, 2 * i * P : 2 * (i + 1) * P].bitcast(E2M1),
                             lhsT_scale=planes[a][:, S + col : S + col + P],
                             rhs=v_words(a, c0, CHUNK),
                             rhs_scale=planes[a][:, c0 : c0 + CHUNK],
@@ -187,15 +197,24 @@ def tile_list_rotor_window_scores_kernel(
             previous = (j, b, n0, h_bf)
         quantise_h(*previous)
 
+        late_codes = keep.tile([P, 4 * P], U32, name="late_codes", tag="wa_raw1", align_bytes=64)
+        late_scales = keep.tile([P, 4 * P], U8, name="late_scales", align_bytes=64)
+        for n, (name, g) in enumerate(grouped):
+            cols = slice(n * P, (n + 1) * P)
+            nc.vector.quantize_mx(
+                late_codes[:, cols].bitcast(E4M3), late_scales[:, cols], grouped[name, g][:, PACK * early :]
+            )
+            w_codes[name, g, PACK - 1] = late_codes[:, cols]
+            w_scales[name, g, PACK - 1] = late_scales[:, cols]
+
         y = keep.tile([P, PACK, W], F32, name="y", align_bytes=64)
         out_rows = out_0.rearrange("(p t) m -> p t m", t=PACK)
         e = {}
 
         def scores(t):
-            e[t] = ring.tile([P, S], F32, name="e", align_bytes=64)
-            cols = slice(t * P, (t + 1) * P)
+            e[t] = keep.tile([P, S], F32, name=f"e{t}", align_bytes=64)
             for j in range(2):
-                bank = psum.tile([P, HALF], F32, name="e_bank", tag=f"bank{(4, 5, 6, 7, 2, 3, 5, 7)[2 * t + j]}")
+                bank = psum.tile([P, HALF], F32, name="e_bank", tag=f"bank{t + PACK * (1 - j)}")
                 passes = [
                     ("wb", g, 0, HALF, v_words(g, j * HALF, HALF), planes[g][:, j * HALF : (j + 1) * HALF])
                     for g in range(2)
@@ -207,38 +226,32 @@ def tile_list_rotor_window_scores_kernel(
                 for n, (name, g, n0, width, rhs, rhs_scale) in enumerate(passes):
                     nc.tensor.matmul_mx(
                         out=bank[:, n0 : n0 + width],
-                        lhsT=w_codes[name, g][:, cols].bitcast(E4M3),
-                        lhsT_scale=w_scales[name, g][:, cols],
+                        lhsT=w_codes[name, g, t].bitcast(E4M3),
+                        lhsT_scale=w_scales[name, g, t],
                         rhs=rhs,
                         rhs_scale=rhs_scale,
                         start=(n == 0),
                         stop=(n == len(passes) - 1),
                     )
-                if j == 1 and t < 2:
-                    nc.vector.tensor_copy(e[t][:, j * HALF : (j + 1) * HALF], bank[:])
-                else:
-                    nc.scalar.copy(e[t][:, j * HALF : (j + 1) * HALF], bank[:])
+                nc.scalar.copy(e[t][:, j * HALF : (j + 1) * HALF], bank[:])
 
-        gate, gap = {}, {}
+        gate, plain, diff, weighted = {}, {}, {}, {}
+
+        def pick(t):
+            plain[t] = keep.tile([P, W], F32, name=f"plain{t}")
+            nc.vector.tensor_copy(plain[t][:], e[t][:].indirect(pos2_sb[:]))
 
         def look(t):
             gate[t] = keep.tile([P, W], F32, name=f"gate{t}")
             nc.scalar.activation(gate[t][:], e[t][:].indirect(pos1_sb[:]), ACT.Sigmoid, bias=vib_sb[:, t : t + 1])
-            diff = keep.tile([P, W], F32, name=f"diff{t}")
-            if t == 0:
-                plain = keep.tile([P, W], F32, name="plain")
-                nc.vector.tensor_copy(plain[:], e[t][:].indirect(pos2_sb[:]))
-                nc.vector.tensor_tensor(diff[:], plain[:], gate[t][:], ALU.subtract)
-            else:
-                nc.vector.tensor_tensor(diff[:], e[t][:].indirect(pos2_sb[:]), gate[t][:], ALU.subtract)
-            gap[t] = keep.tile([P, W], F32, name=f"gap{t}")
-            nc.scalar.activation(gap[t][:], diff[:], ACT.Abs)
-
-        weighted = {}
+            diff[t] = keep.tile([P, W], F32, name=f"diff{t}", tag=f"diff{t}", align_bytes=64)
+            nc.vector.tensor_tensor(diff[t][:], plain[t][:], gate[t][:], ALU.subtract)
 
         def weigh(t):
+            gap = keep.tile([P, W], F32, name=f"gap{t}")
+            nc.scalar.activation(gap[:], diff[t][:], ACT.Abs)
             weighted[t] = keep.tile([P, W], F32, name=f"weighted{t}")
-            nc.vector.tensor_tensor(weighted[t][:], gap[t][:], wear_sb[:, t, :], ALU.mult)
+            nc.vector.tensor_tensor(weighted[t][:], gap[:], wear_sb[:, t, :], ALU.mult)
 
         def finish(t):
             nc.vector.scalar_tensor_tensor(
@@ -246,19 +259,23 @@ def tile_list_rotor_window_scores_kernel(
             )
             nc.sync.dma_start(out_rows[:, t, :], y[:, t, :])
 
-        y_bf = keep.tile([P, W, PACK], BF16, name="y_bf", align_bytes=64)
+        for t in range(PACK):
+            scores(t)
+            pick(t)
+            if t >= 2:
+                weigh(t - 2)
+            look(t)
+            if t >= 2:
+                finish(t - 2)
+        y_bf = keep.tile([P, W, PACK], BF16, name="y_bf", tag=f"diff{PACK - 1}", align_bytes=64)
         y_by_column = y[:].rearrange("p t m -> p m t")
-        for step in range(PACK + 2):
-            if step < PACK:
-                scores(step)
-                look(step)
-            if step >= 2:
-                finish(step - 2)
-            if 1 <= step <= PACK:
-                weigh(step - 1)
-            if step == 3:
-                nc.scalar.copy(y_bf[:, :, 0:2], y_by_column[:, :, 0:2])
-        nc.vector.tensor_copy(y_bf[:, :, 2:4], y_by_column[:, :, 2:4])
+        for t in (2, 3):
+            weigh(t)
+        nc.scalar.copy(y_bf[:, :, 0:2], y_by_column[:, :, 0:2])
+        for t in (2, 3):
+            finish(t)
+        nc.vector.tensor_copy(y_bf[:, :VECTOR_COLUMNS, 2:4], y_by_column[:, :VECTOR_COLUMNS, 2:4])
+        nc.scalar.copy(y_bf[:, VECTOR_COLUMNS:, 2:4], y_by_column[:, VECTOR_COLUMNS:, 2:4])
         y_codes = keep.tile([P, W], U32, name="y_codes", align_bytes=64)
         y_scales = keep.tile([P, W], U8, name="y_scales", align_bytes=64)
         nc.vector.quantize_mx(y_codes[:].bitcast(E4M3), y_scales[:], y_bf[:].rearrange("p m t -> p (m t)"))

from contextlib import ExitStack

import concourse.mybir as mybir

K, T, S, H, N, W = 1024, 4096, 1024, 1024, 512, 512
FLOPS = 2 * K * H * S + 2 * (H + K) * N * S

F32 = mybir.dt.float32
BF16 = mybir.dt.bfloat16
I32 = mybir.dt.int32
U32 = mybir.dt.uint32
U16 = mybir.dt.uint16
U8 = mybir.dt.uint8
E4M3 = mybir.dt.float8_e4m3fn_x4
E2M1 = mybir.dt.float4_e2m1fn_x4
ALU = mybir.AluOpType
ACT = mybir.ActivationFunctionType

P = 128
PACK = 4
PASS = P * PACK
HALF = 512
CHUNK = 128
VECTOR_COLUMNS = 320


def tile_list_rotor_window_scores_kernel(
    tc, tab_words, tab_scales, offs, pos1, pos2, w1_words, w1_scales, low, wa, wb, vib, wear, gain,
    out_0, out_1, out_2,
):
    nc = tc.nc
    with ExitStack() as ctx:
        lists = ctx.enter_context(tc.tile_pool(name="lists", bufs=1))
        keep = ctx.enter_context(tc.tile_pool(name="keep", bufs=1))
        ring = ctx.enter_context(tc.tile_pool(name="ring", bufs=2))
        psum = ctx.enter_context(tc.psum_pool(name="psum", bufs=1))

        offs_sb = lists.tile([P, S // 16], U16, name="offs_sb")
        pos1_sb = lists.tile([P, W // 16], U16, name="pos1_sb")
        pos2_sb = lists.tile([P, W // 16], U16, name="pos2_sb")
        nc.sync.dma_start(offs_sb[:], offs)

        warm_in = keep.tile([P, 1], F32, name="warm_in")
        warm_out = keep.tile([P, 1], F32, name="warm_out")
        nc.gpsimd.memset(warm_in[:], 0.0)
        nc.scalar.activation(warm_out[:], warm_in[:], ACT.Sigmoid)

        tab_s = keep.tile([P, T], U8, name="tab_s", align_bytes=64)
        w1s_raw = keep.tile([P, H], U8, name="w1s_raw", align_bytes=64)
        w1_raw = [keep.tile([P, 2, 2 * PASS], U8, name=f"w1_raw{b}", align_bytes=64) for b in range(2)]
        w1_halves = w1_words.rearrange("a p (b c) -> b p a c", b=2)
        planes = [keep.tile([P, S + H], U8, name=f"planes{a}", align_bytes=64) for a in range(2)]
        tab_w0 = keep.tile([P, T], I32, name="tab_w0", align_bytes=64)
        tab_w1 = keep.tile([P, T], I32, name="tab_w1", align_bytes=64)
        tab_words1 = tab_words[1].rearrange("p t i -> p (t i)").bitcast(I32)
        nc.sync.dma_start(tab_s[0:32, :].bitcast(I32), tab_scales.rearrange("a q t -> (a q) t").bitcast(I32))
        nc.sync.dma_start(w1s_raw[0:32, :].bitcast(I32), w1_scales.rearrange("a q c -> (a q) c").bitcast(I32))
        nc.sync.dma_start(w1_raw[0][:].bitcast(I32), w1_halves[0].bitcast(I32))
        nc.sync.dma_start(tab_w0[:], tab_words[0].rearrange("p t i -> p (t i)").bitcast(I32))
        nc.sync.dma_start(tab_w1[:, : T // 2], tab_words1[:, : T // 2])
        for rows in (slice(32, 64), slice(64, P)):
            nc.vector.memset(tab_s[rows, :].bitcast(I32), 0)
            nc.gpsimd.memset(w1s_raw[rows, :].bitcast(I32), 0)
        nc.gpsimd.memset(planes[1][:].bitcast(I32), 0)

        low_sb = keep.tile([P, 2, 2 * PACK], F32, name="low_sb")
        low_runs = low.rearrange("(b k x) -> k b x", b=2, x=2 * PACK)
        for e in range(2):
            nc.gpsimd.dma_start(low_sb[e:P:2, :, 0:7], low_runs[:, :, e : e + 7])

        picked_s = keep.tile([P, S], U8, name="picked_s", align_bytes=64)
        nc.vector.tensor_copy(picked_s[:], tab_s[:].indirect(offs_sb[:]))
        nc.vector.tensor_copy(planes[0][:, :S].bitcast(I32), picked_s[:].bitcast(I32))
        nc.scalar.copy(
            planes[0][:, S:].bitcast(U16).rearrange("p (b i k) -> p b k i", b=2, i=PACK),
            w1s_raw[:].bitcast(U16).rearrange("p (b k i) -> p b k i", b=2, i=PACK),
        )
        for q in range(1, 4):
            nc.sync.dma_start(
                planes[0][32 * q : 32 * q + 4, :].bitcast(I32), planes[0][4 * q : 4 * q + 4, :].bitcast(I32)
            )
        for q in range(4):
            (nc.gpsimd if q == 0 else nc.sync).dma_start(
                planes[1][32 * q : 32 * q + 4, :].bitcast(I32),
                planes[0][16 + 4 * q : 20 + 4 * q, :].bitcast(I32),
            )
        nc.sync.dma_start(tab_w1[:, T // 2 :], tab_words1[:, T // 2 :])
        nc.sync.dma_start(w1_raw[1][:].bitcast(I32), w1_halves[1].bitcast(I32))

        w1_d = [keep.tile([P, 2, 2 * PASS], U8, name=f"w1_d{b}", align_bytes=64) for b in range(2)]
        for b in range(2):
            nc.scalar.copy(
                w1_d[b][:].bitcast(U32).rearrange("p a (i k) -> p a k i", i=PACK),
                w1_raw[b][:].bitcast(U32).rearrange("p a (k i) -> p a k i", i=PACK),
            )

        v_w = {}
        for a, tab_w in enumerate((tab_w0, tab_w1)):
            for j in range(2):
                v_w[a, j] = keep.tile([P, HALF], U32, name=f"v_w{a}{j}", align_bytes=64)
                nc.vector.tensor_copy(
                    v_w[a, j][:], tab_w[:].bitcast(U32).indirect(offs_sb[:, j * 32 : (j + 1) * 32])
                )

        def v_words(a, c0, n):
            return v_w[a, c0 // HALF][:, c0 % HALF : c0 % HALF + n].bitcast(E4M3)

        raw = {
            (name, g): keep.tile([P, PACK * N], F32, name=f"{name}_raw{g}", tag=f"{name}_raw{g}", align_bytes=64)
            for name in ("wb", "wa")
            for g in range(2)
        }
        for g in range(2):
            nc.sync.dma_start(
                raw["wb", g][:], wb[g * PASS : (g + 1) * PASS, :].rearrange("(p j) n -> p (j n)", j=PACK)
            )
        for g in range(2):
            wa_rows = wa[g * PASS : (g + 1) * PASS, :].rearrange("(k i e) n -> e k i n", i=PACK, e=2)
            for e in range(2):
                nc.sync.dma_start(raw["wa", g][e:P:2, :].rearrange("p (i n) -> p i n", i=PACK), wa_rows[e])
        vib_sb = keep.tile([P, PACK], F32, name="vib_sb")
        gain_sb = keep.tile([P, PACK], F32, name="gain_sb")
        nc.sync.dma_start(vib_sb[:], vib.rearrange("(p t) -> p t", t=PACK))
        nc.sync.dma_start(gain_sb[:], gain.rearrange("(p t) -> p t", t=PACK))
        nc.sync.dma_start(pos1_sb[:], pos1)
        nc.sync.dma_start(pos2_sb[:], pos2)
        wear_sb = keep.tile([P, PACK, W], F32, name="wear_sb", align_bytes=64)
        nc.sync.dma_start(wear_sb[:], wear.rearrange("(p t) m -> p t m", t=PACK))
        neg_gain = keep.tile([P, PACK], F32, name="neg_gain")
        nc.gpsimd.tensor_scalar(neg_gain[:], gain_sb[:], -1.0, 0.0, ALU.mult, ALU.add)

        grouped, w_codes, w_scales = {}, {}, {}
        early = (PACK - 1) * P

        def quantise_weight(name, g):
            grouped[name, g] = keep.tile([P, PACK * N], BF16, name=f"{name}_grouped{g}", align_bytes=64)
            nc.scalar.copy(
                grouped[name, g][:].rearrange("p (t m j) -> p m j t", t=PACK, j=PACK),
                raw[name, g][:].rearrange("p (j m t) -> p m j t", j=PACK, t=PACK),
            )
            codes = keep.tile([P, early], U32, name=f"{name}_codes{g}", align_bytes=64)
            scales = keep.tile([P, early], U8, name=f"{name}_scales{g}", align_bytes=64)
            nc.vector.quantize_mx(codes[:].bitcast(E4M3), scales[:], grouped[name, g][:, : PACK * early])
            for t in range(PACK - 1):
                w_codes[name, g, t] = codes[:, t * P : (t + 1) * P]
                w_scales[name, g, t] = scales[:, t * P : (t + 1) * P]

        h_parts = {}

        def quantise_h(j, b, n0, h_bf):
            width = h_bf.shape[1]
            codes = keep.tile([P, width], U32, name=f"h_codes{j}{b}_{n0}", align_bytes=64)
            scales = keep.tile([P, width], U8, name=f"h_scales{j}{b}_{n0}", align_bytes=64)
            nc.vector.quantize_mx(codes[:].bitcast(E4M3), scales[:], h_bf[:].rearrange("p n i -> p (n i)"))
            h_parts.setdefault((j, b), []).append((n0, width, codes, scales))

        units = [
            (0, 0, 0, HALF, None),
            (1, 0, 0, HALF, ("wb", 0)),
            (0, 1, 0, HALF, ("wb", 1)),
            (1, 1, 0, HALF // 2, ("wa", 0)),
            (1, 1, HALF // 2, HALF // 2, ("wa", 1)),
        ]
        previous = None
        n_bank = 0
        for u, (j, b, n0, width, weight) in enumerate(units):
            if weight is not None:
                quantise_weight(*weight)
            if u == len(units) - 1:
                h_bf = keep.tile([P, width, PACK], BF16, name="h_bf_last", tag="wa_raw1", align_bytes=64)
            else:
                h_bf = ring.tile([P, width, PACK], BF16, name="h_bf", align_bytes=64)
            for c in range(width // CHUNK):
                bank = psum.tile([P, PACK, CHUNK], F32, name="h_bank", tag=f"bank{n_bank if n_bank < 8 else n_bank % 4}")
                n_bank += 1
                c0 = j * HALF + n0 + c * CHUNK
                for a in range(2):
                    for i in range(PACK):
                        col = b * PASS + i * P
                        nc.tensor.matmul_mx(
                            out=bank[:, i, :],
                            lhsT=w1_d[b][:, a, 2 * i * P : 2 * (i + 1) * P].bitcast(E2M1),
                            lhsT_scale=planes[a][:, S + col : S + col + P],
                            rhs=v_words(a, c0, CHUNK),
                            rhs_scale=planes[a][:, c0 : c0 + CHUNK],
                            start=(a == 0 and i == 0),
                            stop=(a == 1 and i == PACK - 1),
                        )
                nc.vector.tensor_tensor(
                    h_bf[:, c * CHUNK : (c + 1) * CHUNK, :],
                    bank[:].rearrange("p i n -> p n i"),
                    low_sb[:, b : b + 1, 0:7:2].to_broadcast([P, CHUNK, PACK]),
                    ALU.max,
                )
                if c == 0 and previous is not None:
                    quantise_h(*previous)
            previous = (j, b, n0, h_bf)
        quantise_h(*previous)

        late_codes = keep.tile([P, 4 * P], U32, name="late_codes", tag="wa_raw1", align_bytes=64)
        late_scales = keep.tile([P, 4 * P], U8, name="late_scales", align_bytes=64)
        for n, (name, g) in enumerate(grouped):
            cols = slice(n * P, (n + 1) * P)
            nc.vector.quantize_mx(
                late_codes[:, cols].bitcast(E4M3), late_scales[:, cols], grouped[name, g][:, PACK * early :]
            )
            w_codes[name, g, PACK - 1] = late_codes[:, cols]
            w_scales[name, g, PACK - 1] = late_scales[:, cols]

        y = keep.tile([P, PACK, W], F32, name="y", align_bytes=64)
        out_rows = out_0.rearrange("(p t) m -> p t m", t=PACK)
        e = {}

        def scores(t):
            e[t] = keep.tile([P, S], F32, name=f"e{t}", align_bytes=64)
            for j in range(2):
                bank = psum.tile([P, HALF], F32, name="e_bank", tag=f"bank{t + PACK * (1 - j)}")
                passes = [
                    ("wb", g, 0, HALF, v_words(g, j * HALF, HALF), planes[g][:, j * HALF : (j + 1) * HALF])
                    for g in range(2)
                ] + [
                    ("wa", g, n0, width, codes[:].bitcast(E4M3), scales[:])
                    for g in range(2)
                    for n0, width, codes, scales in h_parts[j, g]
                ]
                for n, (name, g, n0, width, rhs, rhs_scale) in enumerate(passes):
                    nc.tensor.matmul_mx(
                        out=bank[:, n0 : n0 + width],
                        lhsT=w_codes[name, g, t].bitcast(E4M3),
                        lhsT_scale=w_scales[name, g, t],
                        rhs=rhs,
                        rhs_scale=rhs_scale,
                        start=(n == 0),
                        stop=(n == len(passes) - 1),
                    )
                nc.scalar.copy(e[t][:, j * HALF : (j + 1) * HALF], bank[:])

        gate, plain, diff, weighted = {}, {}, {}, {}

        def pick(t):
            plain[t] = keep.tile([P, W], F32, name=f"plain{t}")
            nc.vector.tensor_copy(plain[t][:], e[t][:].indirect(pos2_sb[:]))

        def look(t):
            gate[t] = keep.tile([P, W], F32, name=f"gate{t}")
            nc.scalar.activation(gate[t][:], e[t][:].indirect(pos1_sb[:]), ACT.Sigmoid, bias=vib_sb[:, t : t + 1])
            diff[t] = keep.tile([P, W], F32, name=f"diff{t}", tag=f"diff{t}", align_bytes=64)
            nc.vector.tensor_tensor(diff[t][:], plain[t][:], gate[t][:], ALU.subtract)

        def weigh(t):
            gap = keep.tile([P, W], F32, name=f"gap{t}")
            nc.scalar.activation(gap[:], diff[t][:], ACT.Abs)
            weighted[t] = keep.tile([P, W], F32, name=f"weighted{t}")
            nc.vector.tensor_tensor(weighted[t][:], gap[:], wear_sb[:, t, :], ALU.mult)

        def finish(t):
            nc.vector.scalar_tensor_tensor(
                y[:, t, :], gate[t][:], neg_gain[:, t : t + 1], weighted[t][:], ALU.mult, ALU.add
            )
            nc.sync.dma_start(out_rows[:, t, :], y[:, t, :])

        for t in range(PACK):
            scores(t)
            pick(t)
            if t >= 2:
                weigh(t - 2)
            look(t)
            if t >= 2:
                finish(t - 2)
        y_bf = keep.tile([P, W, PACK], BF16, name="y_bf", tag=f"diff{PACK - 1}", align_bytes=64)
        y_by_column = y[:].rearrange("p t m -> p m t")
        for t in (2, 3):
            weigh(t)
        nc.scalar.copy(y_bf[:, :, 0:2], y_by_column[:, :, 0:2])
        for t in (2, 3):
            finish(t)
        nc.vector.tensor_copy(y_bf[:, :VECTOR_COLUMNS, 2:4], y_by_column[:, :VECTOR_COLUMNS, 2:4])
        nc.scalar.copy(y_bf[:, VECTOR_COLUMNS:, 2:4], y_by_column[:, VECTOR_COLUMNS:, 2:4])
        y_codes = keep.tile([P, W], U32, name="y_codes", align_bytes=64)
        y_scales = keep.tile([P, W], U8, name="y_scales", align_bytes=64)
        nc.vector.quantize_mx(y_codes[:].bitcast(E4M3), y_scales[:], y_bf[:].rearrange("p m t -> p (m t)"))
        nc.sync.dma_start(out_1[0].rearrange("p m t -> p (m t)").bitcast(I32), y_codes[:].bitcast(I32))
        for q in range(4):
            queue = nc.scalar if q % 2 == 0 else nc.sync
            queue.dma_start(
                out_2[0, 4 * q : 4 * q + 4, :].bitcast(I32), y_scales[32 * q : 32 * q + 4, :].bitcast(I32)
            )
